import numpy as np
import ml_dtypes


def mxq(x, axis, fmt="e4m3"):
    dtype, down = {"e4m3": (ml_dtypes.float8_e4m3fn, 7), "e5m2": (ml_dtypes.float8_e5m2, 14)}[fmt]
    v = np.moveaxis(np.asarray(x, np.float32).astype(ml_dtypes.bfloat16).astype(np.float64), axis, -1)
    blocks = v.reshape(v.shape[:-1] + (-1, 32))
    amax = np.abs(blocks).max(-1, keepdims=True)
    byte = np.maximum(np.where(amax > 0, np.frexp(amax)[1] - 1 + 127, 0) - down, 1)
    scale = np.exp2(byte - 127.0)
    codes = (blocks / scale).astype(np.float32).astype(dtype).astype(np.float64)
    return np.moveaxis((codes * scale).reshape(v.shape), -1, axis)


WIDE = False


def mx_kscale(k):
    if not WIDE:
        return np.ones(k)
    levels = np.array([10, -10, 5, -5, 0])
    if k % 512:
        return np.exp2(np.random.permutation(np.resize(levels, k // 32))).repeat(32)
    a = np.empty((k // 512, 16))
    for p in range(k // 512):
        a[p, :8] = np.random.permutation(np.resize(levels, 8))
        for g in range(8):
            far = levels[np.abs(levels - a[p, g]) >= 10]
            a[p, g + 8] = far[np.random.randint(len(far))]
    return np.exp2(a.ravel()).repeat(32)


def f64(x):
    return np.asarray(x).astype(np.float64)


E2M1 = np.array([0.0, 0.5, 1.0, 1.5, 2.0, 3.0, 4.0, 6.0, -0.0, -0.5, -1.0, -1.5, -2.0, -3.0, -4.0, -6.0])


def pack_weight(w, fmt):
    k, n = w.shape
    w = f64(np.asarray(w, np.float32).astype(ml_dtypes.bfloat16)).reshape(k // 32, 32, n)
    amax = np.abs(w).max(1)
    if fmt == "e4m3":
        byte = np.frexp(amax)[1] - 1 + 127 - 7
    else:
        mant, ex = np.frexp(amax / 6.0)
        byte = np.where(mant > 0.5, ex, ex - 1) + 127
    byte = np.clip(np.where(amax > 0, byte, 1), 1, 254)
    scaled = (w * np.exp2(127.0 - byte)[:, None, :]).reshape(k, n).astype(np.float32)
    by_word = np.ascontiguousarray(scaled.reshape(k // 512, 128, 4, n).transpose(0, 1, 3, 2))
    if fmt == "e4m3":
        words = by_word.astype(ml_dtypes.float8_e4m3fn).view(np.uint8)
    else:
        c = by_word.astype(ml_dtypes.float4_e2m1fn).view(np.uint8) & 0xF
        words = (c[..., 0::2] | (c[..., 1::2] << 4)).reshape(k // 512, 128, 2 * n)
    return np.ascontiguousarray(words), np.ascontiguousarray(byte.astype(np.uint8).reshape(k // 512, 16, n))


def unpack_weight(words, scales, fmt):
    g, _, n = scales.shape
    words = np.ascontiguousarray(words).reshape(g, 128, n, -1)
    if fmt == "e4m3":
        vals = words.view(ml_dtypes.float8_e4m3fn).astype(np.float64)
    else:
        nib = np.empty((g, 128, n, 4), np.uint8)
        nib[..., 0::2] = words & 0xF
        nib[..., 1::2] = words >> 4
        vals = E2M1[nib]
    vals = vals * np.repeat(np.exp2(scales.astype(np.float64) - 127.0), 8, axis=1)[..., None]
    return vals.transpose(0, 1, 3, 2).reshape(g * 512, n)


def planes(y):
    n, m = y.shape
    v = y.astype(np.float32).astype(ml_dtypes.bfloat16).astype(np.float64).reshape(n // 32, 32, m)
    top = np.abs(v).max(1)
    byte = np.clip(np.where(top > 0, np.frexp(top)[1] - 1 + 127 - 7, 1), 1, 254)
    codes = (v * np.exp2(127.0 - byte)[:, None, :]).reshape(n, m).astype(np.float32).astype(ml_dtypes.float8_e4m3fn).view(np.uint8)
    words = codes.reshape(n // 512, 128, 4, m).transpose(0, 1, 3, 2)
    return np.ascontiguousarray(words), np.ascontiguousarray(byte.astype(np.uint8).reshape(n // 512, 16, m))


def silu(v):
    return v / (1.0 + np.exp(-np.maximum(v, -700.0)))


K, M, T = 1024, 512, 512


def setup_inputs():
    n = np.random.standard_normal
    s = mx_kscale(K)[:, None]
    u = mx_kscale(T)[:, None]
    q = n((K, T)) * s
    p_vc = pack_weight(0.1 * n((T, M)) / u, "e2m1")
    return {
        "qc": (q).astype(np.float32),
        "kc": (n((K, T)) / np.sqrt(K) / s).astype(np.float32),
        "qd": (q * 0.995 ** (np.arange(T) + 1.0)).astype(np.float32),
        "st": (n((K, M)) / np.sqrt(K) / s).astype(np.float32),
        "vc_words": p_vc[0],
        "vc_scales": p_vc[1],
        "dm": (np.tril(0.995 ** (np.arange(T)[:, None] - np.arange(T)[None])).T * u).astype(np.float32),
        "b": (0.3 * n(512)).astype(np.float32),
    }


def reference(qc, kc, qd, st, vc_words, vc_scales, dm, b):
    qc_ = mxq(f64(qc), 0, "e4m3")
    kc_ = mxq(f64(kc), 0, "e4m3")
    qd_ = mxq(f64(qd), 0, "e4m3")
    st_ = mxq(f64(st), 0, "e4m3")
    vc_ = unpack_weight(vc_words, vc_scales, "e2m1")
    h_ = mxq((kc_.T @ qc_) * f64(dm), 0, "e4m3")
    y = vc_.T @ h_ + st_.T @ qd_
    out_0 = silu(y + f64(b)[:, None])
    return (out_0,) + planes(out_0)

@@ -1,0 +1,200 @@
+from contextlib import ExitStack
+
+import concourse.mybir as mybir
+
+K, M, T = 1024, 512, 512
+FLOPS = 2 * K * T * T + 2 * T * M * T + 2 * K * M * T
+
+F32 = mybir.dt.float32
+BF16 = mybir.dt.bfloat16
+I32 = mybir.dt.int32
+U32 = mybir.dt.uint32
+U8 = mybir.dt.uint8
+FP8X4 = mybir.dt.float8_e4m3fn_x4
+FP4X4 = mybir.dt.float4_e2m1fn_x4
+ACT = mybir.ActivationFunctionType
+ALU = mybir.AluOpType
+
+P = 128
+PACK = 4
+K_PASS = P * PACK
+TC = 128
+CHUNKS = T // TC
+
+
+def tile_mix_linattn_fm_pl_silu_kernel(tc, qc, kc, qd, st, vc_words, vc_scales, dm, b, out_0, out_1, out_2):
+    nc = tc.nc
+    with ExitStack() as ctx:
+        sb = ctx.enter_context(tc.tile_pool(name="sb", bufs=1))
+        ps = ctx.enter_context(tc.psum_pool(name="ps", bufs=1))
+        ctx.enter_context(tc.manual_schedule())
+
+        def load(name, src, a, c0, c1):
+            raw = sb.tile([P, PACK, c1 - c0], F32, name=name, align_bytes=64)
+            rows = src[a * K_PASS : (a + 1) * K_PASS, :].rearrange("(p j) w -> p j w", j=PACK)
+            nc.sync.dma_start(out=raw[:], in_=rows[:, :, c0:c1])
+            return raw
+
+        def operand(name, width):
+            packed = sb.tile([P, PACK * width], BF16, name=name + "_bf", align_bytes=64)
+            codes = sb.tile([P, width], U32, name=name + "_codes", align_bytes=64)
+            scales = sb.tile([P, width], U8, name=name + "_scales", align_bytes=64)
+            return packed, codes, scales
+
+        def copier(engine):
+            return nc.vector.tensor_copy if engine == "vector" else nc.scalar.copy
+
+        def interleave(engine, raw, r0, op, c0, width):
+            dst = op[0][:, PACK * c0 : PACK * (c0 + width)].rearrange("p (c u j) -> p c j u", u=2, j=PACK)
+            src = raw[:, :, r0 : r0 + width].rearrange("p j (c u) -> p c j u", u=2)
+            copier(engine)(out=dst, in_=src)
+
+        def deal(engine, raw, op, half):
+            dst = op[0][:, 1024 * half : 1024 * (half + 1)].rearrange("p (u m j) -> p m j u", u=2, j=PACK)
+            src = raw[:].rearrange("p j (m h u) -> p h m j u", h=2, u=2)[:, half]
+            copier(engine)(out=dst, in_=src)
+
+        def quantize(op, c0, width):
+            nc.vector.quantize_mx(
+                out=op[1][:, c0 : c0 + width].bitcast(FP8X4),
+                scales=op[2][:, c0 : c0 + width],
+                in_=op[0][:, PACK * c0 : PACK * (c0 + width)],
+            )
+
+        def passes(bank, lhs_codes, lhs_scales, mov, c, start, stop):
+            cols = slice(c * TC, (c + 1) * TC)
+            for r in range(PACK):
+                nc.tensor.matmul_mx(
+                    out=bank[:, r, :],
+                    lhsT=lhs_codes(r),
+                    lhsT_scale=lhs_scales[:, r * P : (r + 1) * P],
+                    rhs=mov[1][:, cols].bitcast(FP8X4),
+                    rhs_scale=mov[2][:, cols],
+                    start=start and r == 0,
+                    stop=stop and r == PACK - 1,
+                )
+
+        def fp8_passes(bank, sta, mov, c, start, stop):
+            passes(bank, lambda r: sta[1][:, r * P : (r + 1) * P].bitcast(FP8X4), sta[2], mov, c, start, stop)
+
+        vs_raw = sb.tile([P, M], U8, name="vs_raw", align_bytes=64)
+        nc.vector.memset(vs_raw[:].bitcast(I32), 0)
+        vw_raw = sb.tile([P, 2 * M], U8, name="vw_raw", align_bytes=64)
+        nc.sync.dma_start(out=vw_raw[:].bitcast(I32), in_=vc_words[0].bitcast(I32))
+        kc_raw = [load("kc_raw0", kc, 0, 0, T)]
+        for q in range(4):
+            nc.scalar.dma_start(
+                out=vs_raw[32 * q : 32 * q + 4, :].bitcast(I32), in_=vc_scales[0][4 * q : 4 * q + 4, :].bitcast(I32)
+            )
+        bias = sb.tile([P, PACK], F32, name="bias")
+        nc.scalar.dma_start(out=bias[:], in_=b.rearrange("(p r) -> p r", r=PACK))
+        kc_raw.append(load("kc_raw1", kc, 1, 0, T))
+        qc_raw = [load("qc_raw%d" % a, qc, a, 0, T) for a in range(2)]
+        dm_raw = load("dm_raw", dm, 0, 0, T)
+        st_raw = [load("st_raw%d" % a, st, a, 0, M) for a in range(2)]
+        qd0a = load("qd0a", qd, 0, 0, 256)
+        qd1a = load("qd1a", qd, 1, 0, 256)
+        qd0b = load("qd0b", qd, 0, 256, 512)
+        qd1c = load("qd1c", qd, 1, 256, 384)
+        qd1d = load("qd1d", qd, 1, 384, 512)
+
+        vw = sb.tile([P, 2 * M], U8, name="vw", align_bytes=64)
+        nc.vector.tensor_copy(
+            out=vw[:].rearrange("p (r m y) -> p r m y", r=PACK, y=2),
+            in_=vw_raw[:].rearrange("p (m r y) -> p r m y", r=PACK, y=2),
+        )
+        vs = sb.tile([P, M], U8, name="vs", align_bytes=64)
+        nc.vector.tensor_copy(
+            out=vs[:].rearrange("p (r m) -> p r m", r=PACK),
+            in_=vs_raw[:].rearrange("p (m r) -> p r m", r=PACK),
+        )
+
+        kq = [operand("kq%d" % a, T) for a in range(2)]
+        qq = [operand("qq%d" % a, T) for a in range(2)]
+        sq = [operand("sq%d" % a, M) for a in range(2)]
+        dq = [operand("dq%d" % a, T) for a in range(2)]
+        hq = operand("hq", T)
+        oq = operand("oq", T)
+        s_bank = [ps.tile([P, PACK, TC], F32, name="s_bank%d" % c) for c in range(CHUNKS)]
+        y_bank = [ps.tile([P, PACK, TC], F32, name="y_bank%d" % c) for c in range(CHUNKS)]
+        res = [sb.tile([P, PACK, TC], F32, name="res%d" % c, align_bytes=64) for c in range(CHUNKS)]
+
+        for a in range(2):
+            deal("scalar", kc_raw[a], kq[a], 1)
+            deal("vector", kc_raw[a], kq[a], 0)
+            quantize(kq[a], 0, T)
+        for a in range(2):
+            interleave("scalar", qc_raw[a], 256, qq[a], 256, 256)
+            interleave("vector", qc_raw[a], 0, qq[a], 0, 256)
+            for half in range(2):
+                quantize(qq[a], 256 * half, 256)
+                for c in (2 * half, 2 * half + 1):
+                    fp8_passes(s_bank[c], kq[a], qq[a], c, a == 0, a == 1)
+
+        def decay(c):
+            nc.vector.tensor_tensor(
+                out=hq[0][:, PACK * TC * c : PACK * TC * (c + 1)].rearrange("p (c u j) -> p c j u", u=2, j=PACK),
+                in0=s_bank[c][:].rearrange("p j (c u) -> p c j u", u=2),
+                in1=dm_raw[:, :, TC * c : TC * (c + 1)].rearrange("p j (c u) -> p c j u", u=2),
+                op=ALU.mult,
+            )
+
+        def value_passes(c):
+            passes(y_bank[c], lambda r: vw[:, 2 * P * r : 2 * P * (r + 1)].bitcast(FP4X4), vs, hq, c, True, False)
+
+        for c in range(CHUNKS):
+            decay(c)
+        for half in range(2):
+            quantize(hq, 256 * half, 256)
+            value_passes(2 * half)
+            value_passes(2 * half + 1)
+
+        out_rows = out_0.rearrange("(p r) t -> p r t", r=PACK)
+        words = out_1[0].rearrange("p t i -> p (t i)").bitcast(I32)
+
+        def finish(c):
+            for r in range(PACK):
+                nc.scalar.activation(out=res[c][:, r, :], in_=y_bank[c][:, r, :], func=ACT.Silu, bias=bias[:, r : r + 1])
+            nc.sync.dma_start(out=out_rows[:, :, c * TC : (c + 1) * TC], in_=res[c][:])
+
+        deal("scalar", st_raw[0], sq[0], 1)
+        deal("vector", st_raw[0], sq[0], 0)
+        quantize(sq[0], 0, M)
+        deal("scalar", st_raw[1], sq[1], 1)
+        deal("vector", st_raw[1], sq[1], 0)
+        interleave("scalar", qd0a, 128, dq[0], 128, 128)
+        interleave("vector", qd0a, 0, dq[0], 0, 128)
+        quantize(sq[1], 0, M)
+        quantize(dq[0], 0, 256)
+        for c in (0, 1):
+            fp8_passes(y_bank[c], sq[0], dq[0], c, False, False)
+        interleave("scalar", qd1a, 128, dq[1], 128, 128)
+        interleave("vector", qd1a, 0, dq[1], 0, 128)
+        quantize(dq[1], 0, 256)
+        for c in (0, 1):
+            fp8_passes(y_bank[c], sq[1], dq[1], c, False, True)
+        interleave("scalar", qd0b, 128, dq[0], 384, 128)
+        interleave("vector", qd0b, 0, dq[0], 256, 128)
+        interleave("vector", qd1c, 0, dq[1], 256, 128)
+        quantize(dq[0], 256, 256)
+        for c in (2, 3):
+            fp8_passes(y_bank[c], sq[0], dq[0], c, False, False)
+        interleave("vector", qd1d, 0, dq[1], 384, 128)
+        for c in (2, 3):
+            quantize(dq[1], c * TC, TC)
+            fp8_passes(y_bank[c], sq[1], dq[1], c, False, True)
+
+        for c in range(CHUNKS):
+            finish(c)
+        for c in range(CHUNKS):
+            interleave("vector", res[c], 0, oq, c * TC, TC)
+            if c >= 1:
+                quantize(oq, (c - 1) * TC, TC)
+        nc.scalar.dma_start(out=words[:, 0 : 3 * TC], in_=oq[1][:, 0 : 3 * TC].bitcast(I32))
+        quantize(oq, 3 * TC, TC)
+        nc.sync.dma_start(out=words[:, 3 * TC : T], in_=oq[1][:, 3 * TC : T].bitcast(I32))
+        for q in range(4):
+            queue = nc.scalar if q % 2 == 0 else nc.sync
+            queue.dma_start(
+                out=out_2[0][4 * q : 4 * q + 4, :].bitcast(I32), in_=oq[2][32 * q : 32 * q + 4, :].bitcast(I32)
+            )

@@ -61,17 +61,17 @@ def tile_mix_linattn_fm_pl_silu_kernel(tc, qc, kc, qd, st, vc_words, vc_scales, 
                 in_=op[0][:, PACK * c0 : PACK * (c0 + width)],
             )
 
-        def passes(bank, lhs_codes, lhs_scales, mov, c, start, stop):
+        def passes(sums, lhs_codes, lhs_scales, mov, c, start, stop):
             cols = slice(c * TC, (c + 1) * TC)
             for r in range(PACK):
                 nc.tensor.matmul_mx(
-                    out=bank[:, r, :],
+                    out=sums[r],
                     lhsT=lhs_codes(r),
                     lhsT_scale=lhs_scales[:, r * P : (r + 1) * P],
                     rhs=mov[1][:, cols].bitcast(FP8X4),
                     rhs_scale=mov[2][:, cols],
-                    start=start and r == 0,
-                    stop=stop and r == PACK - 1,
+                    start=start and (r == 0 or sums is y_sums[-1]),
+                    stop=stop and (r == PACK - 1 or sums is y_sums[-1]),
                 )
 
         def fp8_passes(bank, sta, mov, c, start, stop):
@@ -83,30 +83,29 @@ def tile_mix_linattn_fm_pl_silu_kernel(tc, qc, kc, qd, st, vc_words, vc_scales, 
         nc.sync.dma_start(out=vw_raw[:].bitcast(I32), in_=vc_words[0].bitcast(I32))
         kc_raw = [load("kc_raw0", kc, 0, 0, T)]
         for q in range(4):
-            nc.scalar.dma_start(
+            nc.sync.dma_start(
                 out=vs_raw[32 * q : 32 * q + 4, :].bitcast(I32), in_=vc_scales[0][4 * q : 4 * q + 4, :].bitcast(I32)
             )
         bias = sb.tile([P, PACK], F32, name="bias")
-        nc.scalar.dma_start(out=bias[:], in_=b.rearrange("(p r) -> p r", r=PACK))
+        nc.sync.dma_start(out=bias[:], in_=b.rearrange("(p r) -> p r", r=PACK))
+        warm = sb.tile([P, 2], F32, name="warm")
+        nc.vector.memset(warm[:, 0:1], 0.0)
+        nc.scalar.activation(out=warm[:, 1:2], in_=warm[:, 0:1], func=ACT.Silu)
         kc_raw.append(load("kc_raw1", kc, 1, 0, T))
         qc_raw = [load("qc_raw%d" % a, qc, a, 0, T) for a in range(2)]
         dm_raw = load("dm_raw", dm, 0, 0, T)
         st_raw = [load("st_raw%d" % a, st, a, 0, M) for a in range(2)]
         qd0a = load("qd0a", qd, 0, 0, 256)
         qd1a = load("qd1a", qd, 1, 0, 256)
-        qd0b = load("qd0b", qd, 0, 256, 512)
+        qd0c = load("qd0c", qd, 0, 256, 384)
         qd1c = load("qd1c", qd, 1, 256, 384)
+        qd0d = load("qd0d", qd, 0, 384, 512)
         qd1d = load("qd1d", qd, 1, 384, 512)
 
         vw = sb.tile([P, 2 * M], U8, name="vw", align_bytes=64)
         nc.vector.tensor_copy(
             out=vw[:].rearrange("p (r m y) -> p r m y", r=PACK, y=2),
             in_=vw_raw[:].rearrange("p (m r y) -> p r m y", r=PACK, y=2),
-        )
-        vs = sb.tile([P, M], U8, name="vs", align_bytes=64)
-        nc.vector.tensor_copy(
-            out=vs[:].rearrange("p (r m) -> p r m", r=PACK),
-            in_=vs_raw[:].rearrange("p (m r) -> p r m", r=PACK),
         )
 
         kq = [operand("kq%d" % a, T) for a in range(2)]
@@ -116,20 +115,28 @@ def tile_mix_linattn_fm_pl_silu_kernel(tc, qc, kc, qd, st, vc_words, vc_scales, 
         hq = operand("hq", T)
         oq = operand("oq", T)
         s_bank = [ps.tile([P, PACK, TC], F32, name="s_bank%d" % c) for c in range(CHUNKS)]
-        y_bank = [ps.tile([P, PACK, TC], F32, name="y_bank%d" % c) for c in range(CHUNKS)]
+        y_bank = [ps.tile([P, PACK, TC], F32, name="y_bank%d" % c) for c in range(CHUNKS - 1)]
+        s_sums = [[s_bank[c][:, r, :] for r in range(PACK)] for c in range(CHUNKS)]
+        y_sums = [[y_bank[c][:, r, :] for r in range(PACK)] for c in range(CHUNKS - 1)]
+        y_sums.append([s_bank[r][:, 0, :] for r in range(PACK)])
         res = [sb.tile([P, PACK, TC], F32, name="res%d" % c, align_bytes=64) for c in range(CHUNKS)]
 
         for a in range(2):
             deal("scalar", kc_raw[a], kq[a], 1)
             deal("vector", kc_raw[a], kq[a], 0)
             quantize(kq[a], 0, T)
+        vs = sb.tile([P, M], U8, name="vs", align_bytes=64)
+        nc.vector.tensor_copy(
+            out=vs[:].rearrange("p (r m) -> p r m", r=PACK),
+            in_=vs_raw[:].rearrange("p (m r) -> p r m", r=PACK),
+        )
         for a in range(2):
             interleave("scalar", qc_raw[a], 256, qq[a], 256, 256)
             interleave("vector", qc_raw[a], 0, qq[a], 0, 256)
             for half in range(2):
                 quantize(qq[a], 256 * half, 256)
                 for c in (2 * half, 2 * half + 1):
-                    fp8_passes(s_bank[c], kq[a], qq[a], c, a == 0, a == 1)
+                    fp8_passes(s_sums[c], kq[a], qq[a], c, a == 0, a == 1)
 
         def decay(c):
             nc.vector.tensor_tensor(
@@ -140,25 +147,27 @@ def tile_mix_linattn_fm_pl_silu_kernel(tc, qc, kc, qd, st, vc_words, vc_scales, 
             )
 
         def value_passes(c):
-            passes(y_bank[c], lambda r: vw[:, 2 * P * r : 2 * P * (r + 1)].bitcast(FP4X4), vs, hq, c, True, False)
-
-        for c in range(CHUNKS):
-            decay(c)
-        for half in range(2):
-            quantize(hq, 256 * half, 256)
-            value_passes(2 * half)
-            value_passes(2 * half + 1)
+            passes(y_sums[c], lambda r: vw[:, 2 * P * r : 2 * P * (r + 1)].bitcast(FP4X4), vs, hq, c, True, False)
 
         out_rows = out_0.rearrange("(p r) t -> p r t", r=PACK)
         words = out_1[0].rearrange("p t i -> p (t i)").bitcast(I32)
 
         def finish(c):
             for r in range(PACK):
-                nc.scalar.activation(out=res[c][:, r, :], in_=y_bank[c][:, r, :], func=ACT.Silu, bias=bias[:, r : r + 1])
+                nc.scalar.activation(out=res[c][:, r, :], in_=y_sums[c][r], func=ACT.Silu, bias=bias[:, r : r + 1])
             nc.sync.dma_start(out=out_rows[:, :, c * TC : (c + 1) * TC], in_=res[c][:])
 
+        for c in range(3):
+            decay(c)
+        quantize(hq, 0, 256)
+        value_passes(0)
+        value_passes(1)
+        decay(3)
         deal("scalar", st_raw[0], sq[0], 1)
         deal("vector", st_raw[0], sq[0], 0)
+        quantize(hq, 256, 256)
+        value_passes(2)
+        value_passes(3)
         quantize(sq[0], 0, M)
         deal("scalar", st_raw[1], sq[1], 1)
         deal("vector", st_raw[1], sq[1], 0)
@@ -167,30 +176,36 @@ def tile_mix_linattn_fm_pl_silu_kernel(tc, qc, kc, qd, st, vc_words, vc_scales, 
         quantize(sq[1], 0, M)
         quantize(dq[0], 0, 256)
         for c in (0, 1):
-            fp8_passes(y_bank[c], sq[0], dq[0], c, False, False)
+            fp8_passes(y_sums[c], sq[0], dq[0], c, False, False)
         interleave("scalar", qd1a, 128, dq[1], 128, 128)
         interleave("vector", qd1a, 0, dq[1], 0, 128)
         quantize(dq[1], 0, 256)
         for c in (0, 1):
-            fp8_passes(y_bank[c], sq[1], dq[1], c, False, True)
-        interleave("scalar", qd0b, 128, dq[0], 384, 128)
-        interleave("vector", qd0b, 0, dq[0], 256, 128)
+            fp8_passes(y_sums[c], sq[1], dq[1], c, False, True)
+        interleave("scalar", qd0c, 0, dq[0], 256, 128)
+        finish(0)
+        finish(1)
         interleave("vector", qd1c, 0, dq[1], 256, 128)
-        quantize(dq[0], 256, 256)
-        for c in (2, 3):
-            fp8_passes(y_bank[c], sq[0], dq[0], c, False, False)
+        quantize(dq[0], 256, TC)
+        fp8_passes(y_sums[2], sq[0], dq[0], 2, False, False)
+        quantize(dq[1], 256, TC)
+        fp8_passes(y_sums[2], sq[1], dq[1], 2, False, True)
+        finish(2)
+        interleave("vector", qd0d, 0, dq[0], 384, 128)
         interleave("vector", qd1d, 0, dq[1], 384, 128)
-        for c in (2, 3):
-            quantize(dq[1], c * TC, TC)
-            fp8_passes(y_bank[c], sq[1], dq[1], c, False, True)
+        quantize(dq[0], 384, TC)
+        fp8_passes(y_sums[3], sq[0], dq[0], 3, False, False)
+        quantize(dq[1], 384, TC)
+        fp8_passes(y_sums[3], sq[1], dq[1], 3, False, True)
+        finish(3)
 
-        for c in range(CHUNKS):
-            finish(c)
-        for c in range(CHUNKS):
-            interleave("vector", res[c], 0, oq, c * TC, TC)
-            if c >= 1:
-                quantize(oq, (c - 1) * TC, TC)
-        nc.scalar.dma_start(out=words[:, 0 : 3 * TC], in_=oq[1][:, 0 : 3 * TC].bitcast(I32))
+        interleave("vector", res[0], 0, oq, 0, TC)
+        interleave("vector", res[1], 0, oq, TC, TC)
+        interleave("vector", res[2], 0, oq, 2 * TC, TC)
+        quantize(oq, 0, 2 * TC)
+        quantize(oq, 2 * TC, TC)
+        nc.sync.dma_start(out=words[:, 0 : 3 * TC], in_=oq[1][:, 0 : 3 * TC].bitcast(I32))
+        interleave("vector", res[3], 0, oq, 3 * TC, TC)
         quantize(oq, 3 * TC, TC)
         nc.sync.dma_start(out=words[:, 3 * TC : T], in_=oq[1][:, 3 * TC : T].bitcast(I32))
         for q in range(4):

@@ -70,8 +70,8 @@ def tile_mix_linattn_fm_pl_silu_kernel(tc, qc, kc, qd, st, vc_words, vc_scales, 
                     lhsT_scale=lhs_scales[:, r * P : (r + 1) * P],
                     rhs=mov[1][:, cols].bitcast(FP8X4),
                     rhs_scale=mov[2][:, cols],
-                    start=start and (r == 0 or sums is y_sums[-1]),
-                    stop=stop and (r == PACK - 1 or sums is y_sums[-1]),
+                    start=start and (r == 0 or sums is y_sums[3] or (r == 2 and sums is y_sums[2])),
+                    stop=stop and (r == PACK - 1 or sums is y_sums[3] or (r == 1 and sums is y_sums[2])),
                 )
 
         def fp8_passes(bank, sta, mov, c, start, stop):
@@ -95,12 +95,12 @@ def tile_mix_linattn_fm_pl_silu_kernel(tc, qc, kc, qd, st, vc_words, vc_scales, 
         qc_raw = [load("qc_raw%d" % a, qc, a, 0, T) for a in range(2)]
         dm_raw = load("dm_raw", dm, 0, 0, T)
         st_raw = [load("st_raw%d" % a, st, a, 0, M) for a in range(2)]
-        qd0a = load("qd0a", qd, 0, 0, 256)
-        qd1a = load("qd1a", qd, 1, 0, 256)
-        qd0c = load("qd0c", qd, 0, 256, 384)
-        qd1c = load("qd1c", qd, 1, 256, 384)
-        qd0d = load("qd0d", qd, 0, 384, 512)
-        qd1d = load("qd1d", qd, 1, 384, 512)
+        q0a = load("q0a", qd, 0, 0, 256)
+        qa = load("qa", qd, 1, 0, 256)
+        q0b = load("q0b", qd, 0, 256, 512)
+        qd_raw = {}
+        for c in (2, 3):
+            qd_raw[1, c] = load("qd_raw1%d" % c, qd, 1, c * TC, (c + 1) * TC)
 
         vw = sb.tile([P, 2 * M], U8, name="vw", align_bytes=64)
         nc.vector.tensor_copy(
@@ -115,9 +115,10 @@ def tile_mix_linattn_fm_pl_silu_kernel(tc, qc, kc, qd, st, vc_words, vc_scales, 
         hq = operand("hq", T)
         oq = operand("oq", T)
         s_bank = [ps.tile([P, PACK, TC], F32, name="s_bank%d" % c) for c in range(CHUNKS)]
-        y_bank = [ps.tile([P, PACK, TC], F32, name="y_bank%d" % c) for c in range(CHUNKS - 1)]
+        y_bank = [ps.tile([P, PACK, TC], F32, name="y_bank%d" % c) for c in range(CHUNKS)]
         s_sums = [[s_bank[c][:, r, :] for r in range(PACK)] for c in range(CHUNKS)]
-        y_sums = [[y_bank[c][:, r, :] for r in range(PACK)] for c in range(CHUNKS - 1)]
+        y_sums = [[y_bank[c][:, r, :] for r in range(PACK)] for c in range(2)]
+        y_sums.append([y_bank[2 + r // 2][:, r, :] for r in range(PACK)])
         y_sums.append([s_bank[r][:, 0, :] for r in range(PACK)])
         res = [sb.tile([P, PACK, TC], F32, name="res%d" % c, align_bytes=64) for c in range(CHUNKS)]
 
@@ -169,45 +170,57 @@ def tile_mix_linattn_fm_pl_silu_kernel(tc, qc, kc, qd, st, vc_words, vc_scales, 
         value_passes(2)
         value_passes(3)
         quantize(sq[0], 0, M)
+        def pack(engine, a, c):
+            interleave(engine, qd_raw[a, c], 0, dq[a], c * TC, TC)
+
+        def state(a, c):
+            quantize(dq[a], c * TC, TC)
+            fp8_passes(y_sums[c], sq[a], dq[a], c, False, a == 1)
+
+        def pack_result(engine, c):
+            interleave(engine, res[c], 0, oq, c * TC, TC)
+
+        def hand_on(c0, c1):
+            quantize(oq, c0 * TC, (c1 - c0) * TC)
+
+        def store_words(c0, c1):
+            nc.sync.dma_start(out=words[:, c0 * TC : c1 * TC], in_=oq[1][:, c0 * TC : c1 * TC].bitcast(I32))
+
         deal("scalar", st_raw[1], sq[1], 1)
         deal("vector", st_raw[1], sq[1], 0)
-        interleave("scalar", qd0a, 128, dq[0], 128, 128)
-        interleave("vector", qd0a, 0, dq[0], 0, 128)
-        quantize(sq[1], 0, M)
-        quantize(dq[0], 0, 256)
-        for c in (0, 1):
-            fp8_passes(y_sums[c], sq[0], dq[0], c, False, False)
-        interleave("scalar", qd1a, 128, dq[1], 128, 128)
-        interleave("vector", qd1a, 0, dq[1], 0, 128)
-        quantize(dq[1], 0, 256)
-        for c in (0, 1):
-            fp8_passes(y_sums[c], sq[1], dq[1], c, False, True)
-        interleave("scalar", qd0c, 0, dq[0], 256, 128)
+        quantize(sq[1], 0, 256)
+        interleave("vector", q0a, 0, dq[0], 0, 128)
+        interleave("scalar", q0a, 128, dq[0], 128, 128)
+        quantize(sq[1], 256, 256)
+        state(0, 0)
+        state(0, 1)
+        interleave("vector", qa, 0, dq[1], 0, 128)
+        interleave("scalar", qa, 128, dq[1], 128, 128)
+        state(1, 0)
+        state(1, 1)
+        interleave("vector", q0b, 0, dq[0], 256, 128)
+        interleave("scalar", q0b, 128, dq[0], 384, 128)
         finish(0)
         finish(1)
-        interleave("vector", qd1c, 0, dq[1], 256, 128)
-        quantize(dq[0], 256, TC)
-        fp8_passes(y_sums[2], sq[0], dq[0], 2, False, False)
-        quantize(dq[1], 256, TC)
-        fp8_passes(y_sums[2], sq[1], dq[1], 2, False, True)
-        finish(2)
-        interleave("vector", qd0d, 0, dq[0], 384, 128)
-        interleave("vector", qd1d, 0, dq[1], 384, 128)
+        state(0, 2)
+        pack("vector", 1, 2)
         quantize(dq[0], 384, TC)
+        state(1, 2)
         fp8_passes(y_sums[3], sq[0], dq[0], 3, False, False)
-        quantize(dq[1], 384, TC)
-        fp8_passes(y_sums[3], sq[1], dq[1], 3, False, True)
+        finish(2)
+        pack("vector", 1, 3)
+        pack_result("vector", 0)
+        state(1, 3)
+        pack_result("vector", 1)
+        hand_on(0, 2)
+        pack_result("vector", 2)
         finish(3)
-
-        interleave("vector", res[0], 0, oq, 0, TC)
-        interleave("vector", res[1], 0, oq, TC, TC)
-        interleave("vector", res[2], 0, oq, 2 * TC, TC)
-        quantize(oq, 0, 2 * TC)
-        quantize(oq, 2 * TC, TC)
-        nc.sync.dma_start(out=words[:, 0 : 3 * TC], in_=oq[1][:, 0 : 3 * TC].bitcast(I32))
-        interleave("vector", res[3], 0, oq, 3 * TC, TC)
-        quantize(oq, 3 * TC, TC)
-        nc.sync.dma_start(out=words[:, 3 * TC : T], in_=oq[1][:, 3 * TC : T].bitcast(I32))
+        hand_on(2, 3)
+        store_words(0, 3)
+        interleave("scalar", res[3], 80, oq, 3 * TC + 80, 48)
+        interleave("vector", res[3], 0, oq, 3 * TC, 80)
+        hand_on(3, 4)
+        store_words(3, 4)
         for q in range(4):
             queue = nc.scalar if q % 2 == 0 else nc.sync
             queue.dma_start(

from contextlib import ExitStack

import concourse.mybir as mybir

K, M, T = 1024, 512, 512
FLOPS = 2 * K * T * T + 2 * T * M * T + 2 * K * M * T

F32 = mybir.dt.float32
BF16 = mybir.dt.bfloat16
I32 = mybir.dt.int32
U32 = mybir.dt.uint32
U8 = mybir.dt.uint8
FP8X4 = mybir.dt.float8_e4m3fn_x4
FP4X4 = mybir.dt.float4_e2m1fn_x4
ACT = mybir.ActivationFunctionType
ALU = mybir.AluOpType

P = 128
PACK = 4
K_PASS = P * PACK
TC = 128
CHUNKS = T // TC


def tile_mix_linattn_fm_pl_silu_kernel(tc, qc, kc, qd, st, vc_words, vc_scales, dm, b, out_0, out_1, out_2):
    nc = tc.nc
    with ExitStack() as ctx:
        sb = ctx.enter_context(tc.tile_pool(name="sb", bufs=1))
        ps = ctx.enter_context(tc.psum_pool(name="ps", bufs=1))
        ctx.enter_context(tc.manual_schedule())

        def load(name, src, a, c0, c1):
            raw = sb.tile([P, PACK, c1 - c0], F32, name=name, align_bytes=64)
            rows = src[a * K_PASS : (a + 1) * K_PASS, :].rearrange("(p j) w -> p j w", j=PACK)
            nc.sync.dma_start(out=raw[:], in_=rows[:, :, c0:c1])
            return raw

        def operand(name, width):
            packed = sb.tile([P, PACK * width], BF16, name=name + "_bf", align_bytes=64)
            codes = sb.tile([P, width], U32, name=name + "_codes", align_bytes=64)
            scales = sb.tile([P, width], U8, name=name + "_scales", align_bytes=64)
            return packed, codes, scales

        def copier(engine):
            return nc.vector.tensor_copy if engine == "vector" else nc.scalar.copy

        def interleave(engine, raw, r0, op, c0, width):
            dst = op[0][:, PACK * c0 : PACK * (c0 + width)].rearrange("p (c u j) -> p c j u", u=2, j=PACK)
            src = raw[:, :, r0 : r0 + width].rearrange("p j (c u) -> p c j u", u=2)
            copier(engine)(out=dst, in_=src)

        def deal(engine, raw, op, half):
            dst = op[0][:, 1024 * half : 1024 * (half + 1)].rearrange("p (u m j) -> p m j u", u=2, j=PACK)
            src = raw[:].rearrange("p j (m h u) -> p h m j u", h=2, u=2)[:, half]
            copier(engine)(out=dst, in_=src)

        def quantize(op, c0, width):
            nc.vector.quantize_mx(
                out=op[1][:, c0 : c0 + width].bitcast(FP8X4),
                scales=op[2][:, c0 : c0 + width],
                in_=op[0][:, PACK * c0 : PACK * (c0 + width)],
            )

        def passes(sums, lhs_codes, lhs_scales, mov, c, start, stop):
            cols = slice(c * TC, (c + 1) * TC)
            for r in range(PACK):
                nc.tensor.matmul_mx(
                    out=sums[r],
                    lhsT=lhs_codes(r),
                    lhsT_scale=lhs_scales[:, r * P : (r + 1) * P],
                    rhs=mov[1][:, cols].bitcast(FP8X4),
                    rhs_scale=mov[2][:, cols],
                    start=start and (r == 0 or sums is y_sums[3] or (r == 2 and sums is y_sums[2])),
                    stop=stop and (r == PACK - 1 or sums is y_sums[3] or (r == 1 and sums is y_sums[2])),
                )

        def fp8_passes(bank, sta, mov, c, start, stop):
            passes(bank, lambda r: sta[1][:, r * P : (r + 1) * P].bitcast(FP8X4), sta[2], mov, c, start, stop)

        vs_raw = sb.tile([P, M], U8, name="vs_raw", align_bytes=64)
        nc.vector.memset(vs_raw[:].bitcast(I32), 0)
        vw_raw = sb.tile([P, 2 * M], U8, name="vw_raw", align_bytes=64)
        nc.sync.dma_start(out=vw_raw[:].bitcast(I32), in_=vc_words[0].bitcast(I32))
        kc_raw = [load("kc_raw0", kc, 0, 0, T)]
        for q in range(4):
            nc.sync.dma_start(
                out=vs_raw[32 * q : 32 * q + 4, :].bitcast(I32), in_=vc_scales[0][4 * q : 4 * q + 4, :].bitcast(I32)
            )
        bias = sb.tile([P, PACK], F32, name="bias")
        nc.sync.dma_start(out=bias[:], in_=b.rearrange("(p r) -> p r", r=PACK))
        warm = sb.tile([P, 2], F32, name="warm")
        nc.vector.memset(warm[:, 0:1], 0.0)
        nc.scalar.activation(out=warm[:, 1:2], in_=warm[:, 0:1], func=ACT.Silu)
        kc_raw.append(load("kc_raw1", kc, 1, 0, T))
        qc_raw = [load("qc_raw%d" % a, qc, a, 0, T) for a in range(2)]
        dm_raw = load("dm_raw", dm, 0, 0, T)
        st_raw = [load("st_raw%d" % a, st, a, 0, M) for a in range(2)]
        q0a = load("q0a", qd, 0, 0, 256)
        qa = load("qa", qd, 1, 0, 256)
        q0b = load("q0b", qd, 0, 256, 512)
        qd_raw = {}
        for c in (2, 3):
            qd_raw[1, c] = load("qd_raw1%d" % c, qd, 1, c * TC, (c + 1) * TC)

        vw = sb.tile([P, 2 * M], U8, name="vw", align_bytes=64)
        nc.vector.tensor_copy(
            out=vw[:].rearrange("p (r m y) -> p r m y", r=PACK, y=2),
            in_=vw_raw[:].rearrange("p (m r y) -> p r m y", r=PACK, y=2),
        )

        kq = [operand("kq%d" % a, T) for a in range(2)]
        qq = [operand("qq%d" % a, T) for a in range(2)]
        sq = [operand("sq%d" % a, M) for a in range(2)]
        dq = [operand("dq%d" % a, T) for a in range(2)]
        hq = operand("hq", T)
        oq = operand("oq", T)
        s_bank = [ps.tile([P, PACK, TC], F32, name="s_bank%d" % c) for c in range(CHUNKS)]
        y_bank = [ps.tile([P, PACK, TC], F32, name="y_bank%d" % c) for c in range(CHUNKS)]
        s_sums = [[s_bank[c][:, r, :] for r in range(PACK)] for c in range(CHUNKS)]
        y_sums = [[y_bank[c][:, r, :] for r in range(PACK)] for c in range(2)]
        y_sums.append([y_bank[2 + r // 2][:, r, :] for r in range(PACK)])
        y_sums.append([s_bank[r][:, 0, :] for r in range(PACK)])
        res = [sb.tile([P, PACK, TC], F32, name="res%d" % c, align_bytes=64) for c in range(CHUNKS)]

        for a in range(2):
            deal("scalar", kc_raw[a], kq[a], 1)
            deal("vector", kc_raw[a], kq[a], 0)
            quantize(kq[a], 0, T)
        vs = sb.tile([P, M], U8, name="vs", align_bytes=64)
        nc.vector.tensor_copy(
            out=vs[:].rearrange("p (r m) -> p r m", r=PACK),
            in_=vs_raw[:].rearrange("p (m r) -> p r m", r=PACK),
        )
        for a in range(2):
            interleave("scalar", qc_raw[a], 256, qq[a], 256, 256)
            interleave("vector", qc_raw[a], 0, qq[a], 0, 256)
            for half in range(2):
                quantize(qq[a], 256 * half, 256)
                for c in (2 * half, 2 * half + 1):
                    fp8_passes(s_sums[c], kq[a], qq[a], c, a == 0, a == 1)

        def decay(c):
            nc.vector.tensor_tensor(
                out=hq[0][:, PACK * TC * c : PACK * TC * (c + 1)].rearrange("p (c u j) -> p c j u", u=2, j=PACK),
                in0=s_bank[c][:].rearrange("p j (c u) -> p c j u", u=2),
                in1=dm_raw[:, :, TC * c : TC * (c + 1)].rearrange("p j (c u) -> p c j u", u=2),
                op=ALU.mult,
            )

        def value_passes(c):
            passes(y_sums[c], lambda r: vw[:, 2 * P * r : 2 * P * (r + 1)].bitcast(FP4X4), vs, hq, c, True, False)

        out_rows = out_0.rearrange("(p r) t -> p r t", r=PACK)
        words = out_1[0].rearrange("p t i -> p (t i)").bitcast(I32)

        def finish(c):
            for r in range(PACK):
                nc.scalar.activation(out=res[c][:, r, :], in_=y_sums[c][r], func=ACT.Silu, bias=bias[:, r : r + 1])
            nc.sync.dma_start(out=out_rows[:, :, c * TC : (c + 1) * TC], in_=res[c][:])

        for c in range(3):
            decay(c)
        quantize(hq, 0, 256)
        value_passes(0)
        value_passes(1)
        decay(3)
        deal("scalar", st_raw[0], sq[0], 1)
        deal("vector", st_raw[0], sq[0], 0)
        quantize(hq, 256, 256)
        value_passes(2)
        value_passes(3)
        quantize(sq[0], 0, M)
        def pack(engine, a, c):
            interleave(engine, qd_raw[a, c], 0, dq[a], c * TC, TC)

        def state(a, c):
            quantize(dq[a], c * TC, TC)
            fp8_passes(y_sums[c], sq[a], dq[a], c, False, a == 1)

        def pack_result(engine, c):
            interleave(engine, res[c], 0, oq, c * TC, TC)

        def hand_on(c0, c1):
            quantize(oq, c0 * TC, (c1 - c0) * TC)

        def store_words(c0, c1):
            nc.sync.dma_start(out=words[:, c0 * TC : c1 * TC], in_=oq[1][:, c0 * TC : c1 * TC].bitcast(I32))

        deal("scalar", st_raw[1], sq[1], 1)
        deal("vector", st_raw[1], sq[1], 0)
        quantize(sq[1], 0, 256)
        interleave("vector", q0a, 0, dq[0], 0, 128)
        interleave("scalar", q0a, 128, dq[0], 128, 128)
        quantize(sq[1], 256, 256)
        state(0, 0)
        state(0, 1)
        interleave("vector", qa, 0, dq[1], 0, 128)
        interleave("scalar", qa, 128, dq[1], 128, 128)
        state(1, 0)
        state(1, 1)
        interleave("vector", q0b, 0, dq[0], 256, 128)
        interleave("scalar", q0b, 128, dq[0], 384, 128)
        finish(0)
        finish(1)
        state(0, 2)
        pack("vector", 1, 2)
        quantize(dq[0], 384, TC)
        state(1, 2)
        fp8_passes(y_sums[3], sq[0], dq[0], 3, False, False)
        finish(2)
        pack("vector", 1, 3)
        pack_result("vector", 0)
        state(1, 3)
        pack_result("vector", 1)
        hand_on(0, 2)
        pack_result("vector", 2)
        finish(3)
        hand_on(2, 3)
        store_words(0, 3)
        interleave("scalar", res[3], 80, oq, 3 * TC + 80, 48)
        interleave("vector", res[3], 0, oq, 3 * TC, 80)
        hand_on(3, 4)
        store_words(3, 4)
        for q in range(4):
            queue = nc.scalar if q % 2 == 0 else nc.sync
            queue.dma_start(
                out=out_2[0][4 * q : 4 * q + 4, :].bitcast(I32), in_=oq[2][32 * q : 32 * q + 4, :].bitcast(I32)
            )
